import numpy as np
import ml_dtypes


def mxq(x, axis, fmt="e4m3"):
    dtype, down = {"e4m3": (ml_dtypes.float8_e4m3fn, 7), "e5m2": (ml_dtypes.float8_e5m2, 14)}[fmt]
    v = np.moveaxis(np.asarray(x, np.float32).astype(ml_dtypes.bfloat16).astype(np.float64), axis, -1)
    blocks = v.reshape(v.shape[:-1] + (-1, 32))
    amax = np.abs(blocks).max(-1, keepdims=True)
    byte = np.maximum(np.where(amax > 0, np.frexp(amax)[1] - 1 + 127, 0) - down, 1)
    scale = np.exp2(byte - 127.0)
    codes = (blocks / scale).astype(np.float32).astype(dtype).astype(np.float64)
    return np.moveaxis((codes * scale).reshape(v.shape), -1, axis)


WIDE = False


def mx_kscale(k):
    if not WIDE:
        return np.ones(k)
    levels = np.array([10, -10, 5, -5, 0])
    if k % 512:
        return np.exp2(np.random.permutation(np.resize(levels, k // 32))).repeat(32)
    a = np.empty((k // 512, 16))
    for p in range(k // 512):
        a[p, :8] = np.random.permutation(np.resize(levels, 8))
        for g in range(8):
            far = levels[np.abs(levels - a[p, g]) >= 10]
            a[p, g + 8] = far[np.random.randint(len(far))]
    return np.exp2(a.ravel()).repeat(32)


def f64(x):
    return np.asarray(x).astype(np.float64)


def striped(idx):
    return np.tile(idx.reshape(-1, 16).T, (8, 1)).astype(np.uint16)


def unstriped(offs):
    return offs[:16].T.reshape(-1).astype(np.int64)


def relu(v):
    return np.maximum(v, 0.0)


K, T, D, S, V, N = 512, 2048, 4, 512, 128, 256


def setup_inputs():
    n = np.random.standard_normal
    s = mx_kscale(K)[:, None]
    return {
        "xT": (n((K, T)) * s).astype(np.float32),
        "w": (n((K, N)) / np.sqrt(K) / s).astype(np.float32),
        "b": (0.3 * n((N, 1))).astype(np.float32),
        "offs": striped(np.random.permutation(T)[:S]),
    }


def reference(xT, w, b, offs):
    idx = unstriped(offs)
    xq = mxq(f64(xT)[:, idx], 0, "e4m3")
    y = mxq(f64(w), 0, "e4m3").T @ xq
    y = relu(y + f64(b))
    return y.reshape(N, V, D).max(axis=2)

@@ -1,0 +1,93 @@
+from contextlib import ExitStack
+
+import concourse.mybir as mybir
+
+K, T, D, S, V, N = 512, 2048, 4, 512, 128, 256
+P = 128
+PACK = 4
+FLOPS = 2 * K * S * N
+
+F32 = mybir.dt.float32
+BF16 = mybir.dt.bfloat16
+U32 = mybir.dt.uint32
+U16 = mybir.dt.uint16
+U8 = mybir.dt.uint8
+FP8X4 = mybir.dt.float8_e4m3fn_x4
+RELU = mybir.ActivationFunctionType.Relu
+ADD = mybir.AluOpType.add
+MAX = mybir.AluOpType.max
+AXIS_X = mybir.AxisListType.X
+
+HALF = S // 2
+LIST_COLS = S // 16
+
+
+def tile_picked_pool_lin_relu_sub_e_kernel(tc, xT, w, b, offs, out):
+    nc = tc.nc
+    with ExitStack() as ctx:
+        keep = ctx.enter_context(tc.tile_pool(name="keep", bufs=1))
+        psum = ctx.enter_context(tc.psum_pool(name="psum", bufs=1))
+
+        offsets = keep.tile([P, LIST_COLS], U16, name="offsets")
+        planes = [keep.tile([P, T], F32, name=f"plane{t}", align_bytes=64) for t in range(PACK)]
+        w_raw = keep.tile([P, PACK, N], F32, name="w_raw", align_bytes=64)
+        bias = keep.tile([P, 2], F32, name="bias")
+
+        x_rows = xT.rearrange("(p j) t -> p j t", j=PACK)
+        nc.sync.dma_start(planes[0][:], x_rows[:, 0, :])
+        nc.sync.dma_start(offsets[:], offs)
+        for t in range(1, PACK):
+            nc.sync.dma_start(planes[t][:], x_rows[:, t, :])
+        nc.sync.dma_start(w_raw[:], w.rearrange("(p j) m -> p j m", j=PACK))
+        nc.sync.dma_start(bias[:], b.rearrange("(h p) o -> p (h o)", p=P))
+
+        x_grouped = keep.tile([P, S, PACK], BF16, name="x_grouped", align_bytes=64)
+        x_codes = keep.tile([P, S], U32, name="x_codes", align_bytes=64)
+        x_scales = keep.tile([P, S], U8, name="x_scales", align_bytes=64)
+        w_grouped = keep.tile([P, N, PACK], BF16, name="w_grouped", align_bytes=64)
+        w_codes = keep.tile([P, N], U32, name="w_codes", align_bytes=64)
+        w_scales = keep.tile([P, N], U8, name="w_scales", align_bytes=64)
+
+        for t in range(PACK - 1):
+            nc.vector.tensor_copy(x_grouped[:, :, t], planes[t][:].indirect(offsets[:]))
+        for h in range(2):
+            cols = slice(h * HALF, (h + 1) * HALF)
+            lcols = slice(h * LIST_COLS // 2, (h + 1) * LIST_COLS // 2)
+            nc.vector.tensor_copy(x_grouped[:, cols, PACK - 1], planes[PACK - 1][:].indirect(offsets[:, lcols]))
+        for h in range(2):
+            m = slice(h * P, (h + 1) * P)
+            nc.scalar.copy(w_grouped[:, m, :], w_raw[:, :, m].rearrange("p j m -> p m j"))
+        for h in range(2):
+            cols = slice(h * HALF, (h + 1) * HALF)
+            nc.vector.quantize_mx(
+                out=x_codes[:, cols].bitcast(FP8X4),
+                scales=x_scales[:, cols],
+                in_=x_grouped[:, cols, :].rearrange("p n j -> p (n j)"),
+            )
+        accs = []
+        for h in range(2):
+            m = slice(h * P, (h + 1) * P)
+            nc.vector.quantize_mx(
+                out=w_codes[:, m].bitcast(FP8X4),
+                scales=w_scales[:, m],
+                in_=w_grouped[:, m, :].rearrange("p n j -> p (n j)"),
+            )
+            acc = psum.tile([P, S], F32, name=f"acc{h}")
+            nc.tensor.matmul_mx(
+                out=acc[:],
+                lhsT=w_codes[:, m].bitcast(FP8X4),
+                lhsT_scale=w_scales[:, m],
+                rhs=x_codes[:].bitcast(FP8X4),
+                rhs_scale=x_scales[:],
+                start=True,
+                stop=True,
+            )
+            accs.append(acc)
+        for h in range(2):
+            pooled = keep.tile([P, V], F32, name=f"pooled{h}")
+            nc.vector.tensor_reduce(
+                out=pooled[:], in_=accs[h][:].rearrange("p (v d) -> p v d", d=D), axis=AXIS_X, op=MAX
+            )
+            result = keep.tile([P, V], F32, name=f"result{h}")
+            nc.scalar.activation(result[:], pooled[:], RELU, bias=bias[:, h : h + 1])
+            nc.sync.dma_start(out[h * P : (h + 1) * P, :], result[:])

@@ -14,6 +14,7 @@ U16 = mybir.dt.uint16
 U8 = mybir.dt.uint8
 FP8X4 = mybir.dt.float8_e4m3fn_x4
 RELU = mybir.ActivationFunctionType.Relu
+COPY = mybir.ActivationFunctionType.Copy
 ADD = mybir.AluOpType.add
 MAX = mybir.AluOpType.max
 AXIS_X = mybir.AxisListType.X
@@ -32,62 +33,114 @@ def tile_picked_pool_lin_relu_sub_e_kernel(tc, xT, w, b, offs, out):
         planes = [keep.tile([P, T], F32, name=f"plane{t}", align_bytes=64) for t in range(PACK)]
         w_raw = keep.tile([P, PACK, N], F32, name="w_raw", align_bytes=64)
         bias = keep.tile([P, 2], F32, name="bias")
-
-        x_rows = xT.rearrange("(p j) t -> p j t", j=PACK)
-        nc.sync.dma_start(planes[0][:], x_rows[:, 0, :])
-        nc.sync.dma_start(offsets[:], offs)
-        for t in range(1, PACK):
-            nc.sync.dma_start(planes[t][:], x_rows[:, t, :])
-        nc.sync.dma_start(w_raw[:], w.rearrange("(p j) m -> p j m", j=PACK))
-        nc.sync.dma_start(bias[:], b.rearrange("(h p) o -> p (h o)", p=P))
-
-        x_grouped = keep.tile([P, S, PACK], BF16, name="x_grouped", align_bytes=64)
+        x_grouped = [keep.tile([P, HALF, PACK], BF16, name=f"x_grouped{h}", align_bytes=64) for h in range(2)]
         x_codes = keep.tile([P, S], U32, name="x_codes", align_bytes=64)
         x_scales = keep.tile([P, S], U8, name="x_scales", align_bytes=64)
-        w_grouped = keep.tile([P, N, PACK], BF16, name="w_grouped", align_bytes=64)
+        w_grouped = [keep.tile([P, P, PACK], BF16, name=f"w_grouped{h}", align_bytes=64) for h in range(2)]
         w_codes = keep.tile([P, N], U32, name="w_codes", align_bytes=64)
         w_scales = keep.tile([P, N], U8, name="w_scales", align_bytes=64)
+        accs = [[psum.tile([P, HALF], F32, name=f"acc{m}{h}") for h in range(2)] for m in range(2)]
+        pooled = [keep.tile([P, V], F32, name=f"pooled{h}") for h in range(2)]
+        partner = [keep.tile([P, V // 2, 2], F32, name=f"partner{h}") for h in range(2)]
+        pairs = [keep.tile([P, V // 2, 2], F32, name=f"pairs{h}") for h in range(2)]
+        result = [keep.tile([P, V], F32, name=f"result{h}") for h in range(2)]
 
-        for t in range(PACK - 1):
-            nc.vector.tensor_copy(x_grouped[:, :, t], planes[t][:].indirect(offsets[:]))
-        for h in range(2):
-            cols = slice(h * HALF, (h + 1) * HALF)
-            lcols = slice(h * LIST_COLS // 2, (h + 1) * LIST_COLS // 2)
-            nc.vector.tensor_copy(x_grouped[:, cols, PACK - 1], planes[PACK - 1][:].indirect(offsets[:, lcols]))
-        for h in range(2):
-            m = slice(h * P, (h + 1) * P)
-            nc.scalar.copy(w_grouped[:, m, :], w_raw[:, :, m].rearrange("p j m -> p m j"))
-        for h in range(2):
-            cols = slice(h * HALF, (h + 1) * HALF)
+        x_rows = xT.rearrange("(p j) t -> p j t", j=PACK)
+        lcols = [slice(h * LIST_COLS // 2, (h + 1) * LIST_COLS // 2) for h in range(2)]
+        cols = [slice(h * HALF, (h + 1) * HALF) for h in range(2)]
+        vcols = [slice(h * V // 2, (h + 1) * V // 2) for h in range(2)]
+        mcols = [slice(h * P, (h + 1) * P) for h in range(2)]
+        chunks = [[0,2048]]
+        w_rows = w.rearrange("(p j) m -> p j m", j=PACK)
+        nc.sync.dma_start(planes[0][:], x_rows[:, 0, :])
+        nc.sync.dma_start(offsets[:], offs)
+        for t in (2, 3):
+            nc.sync.dma_start(planes[t][:], x_rows[:, t, :])
+        for a, z in chunks:
+            nc.sync.dma_start(planes[1][:, a:z], x_rows[:, 1, a:z])
+        nc.sync.dma_start(w_raw[:], w_rows)
+        nc.sync.dma_start(bias[:], b.rearrange("(h p) o -> p (h o)", p=P))
+
+        def gather(h, t):
+            nc.vector.tensor_copy(x_grouped[h][:, :, t], planes[t][:].indirect(offsets[:, lcols[h]]))
+
+        def quantize_x(h):
             nc.vector.quantize_mx(
-                out=x_codes[:, cols].bitcast(FP8X4),
-                scales=x_scales[:, cols],
-                in_=x_grouped[:, cols, :].rearrange("p n j -> p (n j)"),
+                out=x_codes[:, cols[h]].bitcast(FP8X4),
+                scales=x_scales[:, cols[h]],
+                in_=x_grouped[h][:].rearrange("p n j -> p (n j)"),
             )
-        accs = []
-        for h in range(2):
-            m = slice(h * P, (h + 1) * P)
+
+        def quantize_w(h):
             nc.vector.quantize_mx(
-                out=w_codes[:, m].bitcast(FP8X4),
-                scales=w_scales[:, m],
-                in_=w_grouped[:, m, :].rearrange("p n j -> p (n j)"),
+                out=w_codes[:, mcols[h]].bitcast(FP8X4),
+                scales=w_scales[:, mcols[h]],
+                in_=w_grouped[h][:].rearrange("p n j -> p (n j)"),
             )
-            acc = psum.tile([P, S], F32, name=f"acc{h}")
+
+        def product(m, h):
             nc.tensor.matmul_mx(
-                out=acc[:],
-                lhsT=w_codes[:, m].bitcast(FP8X4),
-                lhsT_scale=w_scales[:, m],
-                rhs=x_codes[:].bitcast(FP8X4),
-                rhs_scale=x_scales[:],
+                out=accs[m][h][:],
+                lhsT=w_codes[:, mcols[m]].bitcast(FP8X4),
+                lhsT_scale=w_scales[:, mcols[m]],
+                rhs=x_codes[:, cols[h]].bitcast(FP8X4),
+                rhs_scale=x_scales[:, cols[h]],
                 start=True,
                 stop=True,
             )
-            accs.append(acc)
-        for h in range(2):
-            pooled = keep.tile([P, V], F32, name=f"pooled{h}")
-            nc.vector.tensor_reduce(
-                out=pooled[:], in_=accs[h][:].rearrange("p (v d) -> p v d", d=D), axis=AXIS_X, op=MAX
+
+        def grouped_sums(m, h):
+            return accs[m][h][:].rearrange("p (v d) -> p v d", d=D)
+
+        def w_view(h):
+            return w_raw[:, :, mcols[h]].rearrange("p j m -> p m j")
+
+        def w_copy_s(m):
+            nc.scalar.copy(
+                w_grouped[m][:].rearrange("p (c i) j -> p c j i", i=4),
+                w_raw[:, :, mcols[m]].rearrange("p j (c i) -> p c j i", i=4),
             )
-            result = keep.tile([P, V], F32, name=f"result{h}")
-            nc.scalar.activation(result[:], pooled[:], RELU, bias=bias[:, h : h + 1])
-            nc.sync.dma_start(out[h * P : (h + 1) * P, :], result[:])
+
+        def w_copy_v(m):
+            nc.vector.tensor_copy(w_grouped[m][:], w_view(m))
+
+        def largest(m, h):
+            nc.vector.tensor_reduce(out=pooled[m][:, vcols[h]], in_=grouped_sums(m, h), axis=AXIS_X, op=MAX)
+
+        def finish(m, h):
+            nc.scalar.activation(result[m][:, vcols[h]], pooled[m][:, vcols[h]], RELU, bias=bias[:, m : m + 1])
+
+        def partners(m, h):
+            nc.scalar.activation(partner[h][:], grouped_sums(m, h)[:, :, 2:4], RELU, bias=bias[:, m : m + 1])
+
+        def pair_up(m, h):
+            nc.vector.scalar_tensor_tensor(
+                pairs[h][:], grouped_sums(m, h)[:, :, 0:2], bias[:, m : m + 1], partner[h][:], op0=ADD, op1=MAX
+            )
+
+        def join(m, h):
+            nc.vector.tensor_tensor(result[m][:, vcols[h]], pairs[h][:, :, 0], pairs[h][:, :, 1], MAX)
+
+        def store(m):
+            nc.sync.dma_start(out[m * P : (m + 1) * P, :], result[m][:])
+
+        gather(0, 0)
+        gather(1, 0)
+        for t in (2, 3, 1):
+            gather(0, t)
+            gather(1, t)
+        w_copy_s(0)
+        w_copy_s(1)
+        quantize_x(0)
+        quantize_w(0)
+        product(0, 0)
+        quantize_x(1)
+        product(0, 1)
+        quantize_w(1)
+        product(1, 0)
+        product(1, 1)
+        for m in range(2):
+            for h in range(2):
+                largest(m, h)
+                finish(m, h)
+            store(m)

@@ -1,6 +1,7 @@
 from contextlib import ExitStack
 
 import concourse.mybir as mybir
+from concourse.masks import make_identity
 
 K, T, D, S, V, N = 512, 2048, 4, 512, 128, 256
 P = 128
@@ -41,8 +42,6 @@ def tile_picked_pool_lin_relu_sub_e_kernel(tc, xT, w, b, offs, out):
         w_scales = keep.tile([P, N], U8, name="w_scales", align_bytes=64)
         accs = [[psum.tile([P, HALF], F32, name=f"acc{m}{h}") for h in range(2)] for m in range(2)]
         pooled = [keep.tile([P, V], F32, name=f"pooled{h}") for h in range(2)]
-        partner = [keep.tile([P, V // 2, 2], F32, name=f"partner{h}") for h in range(2)]
-        pairs = [keep.tile([P, V // 2, 2], F32, name=f"pairs{h}") for h in range(2)]
         result = [keep.tile([P, V], F32, name=f"result{h}") for h in range(2)]
 
         x_rows = xT.rearrange("(p j) t -> p j t", j=PACK)
@@ -60,6 +59,14 @@ def tile_picked_pool_lin_relu_sub_e_kernel(tc, xT, w, b, offs, out):
             nc.sync.dma_start(planes[1][:, a:z], x_rows[:, 1, a:z])
         nc.sync.dma_start(w_raw[:], w_rows)
         nc.sync.dma_start(bias[:], b.rearrange("(h p) o -> p (h o)", p=P))
+
+        identity = keep.tile([P, P], F32, name="identity")
+        make_identity(nc, identity[:])
+        warm = psum.tile([P, 4, P], F32, name="warm")
+
+        def warm_up(n):
+            for i in range(n):
+                nc.tensor.transpose(warm[:, i % 4, :], planes[1][:, i * P : (i + 1) * P], identity[:])
 
         def gather(h, t):
             nc.vector.tensor_copy(x_grouped[h][:, :, t], planes[t][:].indirect(offsets[:, lcols[h]]))
@@ -92,34 +99,17 @@ def tile_picked_pool_lin_relu_sub_e_kernel(tc, xT, w, b, offs, out):
         def grouped_sums(m, h):
             return accs[m][h][:].rearrange("p (v d) -> p v d", d=D)
 
-        def w_view(h):
-            return w_raw[:, :, mcols[h]].rearrange("p j m -> p m j")
-
         def w_copy_s(m):
             nc.scalar.copy(
                 w_grouped[m][:].rearrange("p (c i) j -> p c j i", i=4),
                 w_raw[:, :, mcols[m]].rearrange("p j (c i) -> p c j i", i=4),
             )
 
-        def w_copy_v(m):
-            nc.vector.tensor_copy(w_grouped[m][:], w_view(m))
-
         def largest(m, h):
             nc.vector.tensor_reduce(out=pooled[m][:, vcols[h]], in_=grouped_sums(m, h), axis=AXIS_X, op=MAX)
 
         def finish(m, h):
             nc.scalar.activation(result[m][:, vcols[h]], pooled[m][:, vcols[h]], RELU, bias=bias[:, m : m + 1])
-
-        def partners(m, h):
-            nc.scalar.activation(partner[h][:], grouped_sums(m, h)[:, :, 2:4], RELU, bias=bias[:, m : m + 1])
-
-        def pair_up(m, h):
-            nc.vector.scalar_tensor_tensor(
-                pairs[h][:], grouped_sums(m, h)[:, :, 0:2], bias[:, m : m + 1], partner[h][:], op0=ADD, op1=MAX
-            )
-
-        def join(m, h):
-            nc.vector.tensor_tensor(result[m][:, vcols[h]], pairs[h][:, :, 0], pairs[h][:, :, 1], MAX)
 
         def store(m):
             nc.sync.dma_start(out[m * P : (m + 1) * P, :], result[m][:])
@@ -129,6 +119,7 @@ def tile_picked_pool_lin_relu_sub_e_kernel(tc, xT, w, b, offs, out):
         for t in (2, 3, 1):
             gather(0, t)
             gather(1, t)
+        warm_up(12)
         w_copy_s(0)
         w_copy_s(1)
         quantize_x(0)

@@ -33,6 +33,9 @@ def tile_picked_pool_lin_relu_sub_e_kernel(tc, xT, w, b, offs, out):
         offsets = keep.tile([P, LIST_COLS], U16, name="offsets")
         planes = [keep.tile([P, T], F32, name=f"plane{t}", align_bytes=64) for t in range(PACK)]
         w_raw = keep.tile([P, PACK, N], F32, name="w_raw", align_bytes=64)
+        identity = keep.tile([P, P], F32, name="identity")
+        bias_rows = keep.tile([P, P], F32, name="bias_rows")
+        bias_turned = psum.tile([P, P], F32, name="bias_turned")
         bias = keep.tile([P, 2], F32, name="bias")
         x_grouped = [keep.tile([P, HALF, PACK], BF16, name=f"x_grouped{h}", align_bytes=64) for h in range(2)]
         x_codes = keep.tile([P, S], U32, name="x_codes", align_bytes=64)
@@ -53,20 +56,15 @@ def tile_picked_pool_lin_relu_sub_e_kernel(tc, xT, w, b, offs, out):
         w_rows = w.rearrange("(p j) m -> p j m", j=PACK)
         nc.sync.dma_start(planes[0][:], x_rows[:, 0, :])
         nc.sync.dma_start(offsets[:], offs)
+        nc.gpsimd.memset(bias_rows[:], 0.0)
         for t in (2, 3):
             nc.sync.dma_start(planes[t][:], x_rows[:, t, :])
         for a, z in chunks:
             nc.sync.dma_start(planes[1][:, a:z], x_rows[:, 1, a:z])
         nc.sync.dma_start(w_raw[:], w_rows)
-        nc.sync.dma_start(bias[:], b.rearrange("(h p) o -> p (h o)", p=P))
+        nc.sync.dma_start(bias_rows[0:2, :], b.rearrange("(h p) o -> h (p o)", p=P))
 
-        identity = keep.tile([P, P], F32, name="identity")
         make_identity(nc, identity[:])
-        warm = psum.tile([P, 4, P], F32, name="warm")
-
-        def warm_up(n):
-            for i in range(n):
-                nc.tensor.transpose(warm[:, i % 4, :], planes[1][:, i * P : (i + 1) * P], identity[:])
 
         def gather(h, t):
             nc.vector.tensor_copy(x_grouped[h][:, :, t], planes[t][:].indirect(offsets[:, lcols[h]]))
@@ -119,7 +117,6 @@ def tile_picked_pool_lin_relu_sub_e_kernel(tc, xT, w, b, offs, out):
         for t in (2, 3, 1):
             gather(0, t)
             gather(1, t)
-        warm_up(12)
         w_copy_s(0)
         w_copy_s(1)
         quantize_x(0)
@@ -128,6 +125,8 @@ def tile_picked_pool_lin_relu_sub_e_kernel(tc, xT, w, b, offs, out):
         quantize_x(1)
         product(0, 1)
         quantize_w(1)
+        nc.tensor.transpose(bias_turned[:], bias_rows[:], identity[:])
+        nc.scalar.copy(bias[:], bias_turned[:, 0:2])
         product(1, 0)
         product(1, 1)
         for m in range(2):

from contextlib import ExitStack

import concourse.mybir as mybir
from concourse.masks import make_identity

K, T, D, S, V, N = 512, 2048, 4, 512, 128, 256
P = 128
PACK = 4
FLOPS = 2 * K * S * N

F32 = mybir.dt.float32
BF16 = mybir.dt.bfloat16
U32 = mybir.dt.uint32
U16 = mybir.dt.uint16
U8 = mybir.dt.uint8
FP8X4 = mybir.dt.float8_e4m3fn_x4
RELU = mybir.ActivationFunctionType.Relu
COPY = mybir.ActivationFunctionType.Copy
ADD = mybir.AluOpType.add
MAX = mybir.AluOpType.max
AXIS_X = mybir.AxisListType.X

HALF = S // 2
LIST_COLS = S // 16


def tile_picked_pool_lin_relu_sub_e_kernel(tc, xT, w, b, offs, out):
    nc = tc.nc
    with ExitStack() as ctx:
        keep = ctx.enter_context(tc.tile_pool(name="keep", bufs=1))
        psum = ctx.enter_context(tc.psum_pool(name="psum", bufs=1))

        offsets = keep.tile([P, LIST_COLS], U16, name="offsets")
        planes = [keep.tile([P, T], F32, name=f"plane{t}", align_bytes=64) for t in range(PACK)]
        w_raw = keep.tile([P, PACK, N], F32, name="w_raw", align_bytes=64)
        identity = keep.tile([P, P], F32, name="identity")
        bias_rows = keep.tile([P, P], F32, name="bias_rows")
        bias_turned = psum.tile([P, P], F32, name="bias_turned")
        bias = keep.tile([P, 2], F32, name="bias")
        x_grouped = [keep.tile([P, HALF, PACK], BF16, name=f"x_grouped{h}", align_bytes=64) for h in range(2)]
        x_codes = keep.tile([P, S], U32, name="x_codes", align_bytes=64)
        x_scales = keep.tile([P, S], U8, name="x_scales", align_bytes=64)
        w_grouped = [keep.tile([P, P, PACK], BF16, name=f"w_grouped{h}", align_bytes=64) for h in range(2)]
        w_codes = keep.tile([P, N], U32, name="w_codes", align_bytes=64)
        w_scales = keep.tile([P, N], U8, name="w_scales", align_bytes=64)
        accs = [[psum.tile([P, HALF], F32, name=f"acc{m}{h}") for h in range(2)] for m in range(2)]
        pooled = [keep.tile([P, V], F32, name=f"pooled{h}") for h in range(2)]
        result = [keep.tile([P, V], F32, name=f"result{h}") for h in range(2)]

        x_rows = xT.rearrange("(p j) t -> p j t", j=PACK)
        lcols = [slice(h * LIST_COLS // 2, (h + 1) * LIST_COLS // 2) for h in range(2)]
        cols = [slice(h * HALF, (h + 1) * HALF) for h in range(2)]
        vcols = [slice(h * V // 2, (h + 1) * V // 2) for h in range(2)]
        mcols = [slice(h * P, (h + 1) * P) for h in range(2)]
        chunks = [[0,2048]]
        w_rows = w.rearrange("(p j) m -> p j m", j=PACK)
        nc.sync.dma_start(planes[0][:], x_rows[:, 0, :])
        nc.sync.dma_start(offsets[:], offs)
        nc.gpsimd.memset(bias_rows[:], 0.0)
        for t in (2, 3):
            nc.sync.dma_start(planes[t][:], x_rows[:, t, :])
        for a, z in chunks:
            nc.sync.dma_start(planes[1][:, a:z], x_rows[:, 1, a:z])
        nc.sync.dma_start(w_raw[:], w_rows)
        nc.sync.dma_start(bias_rows[0:2, :], b.rearrange("(h p) o -> h (p o)", p=P))

        make_identity(nc, identity[:])

        def gather(h, t):
            nc.vector.tensor_copy(x_grouped[h][:, :, t], planes[t][:].indirect(offsets[:, lcols[h]]))

        def quantize_x(h):
            nc.vector.quantize_mx(
                out=x_codes[:, cols[h]].bitcast(FP8X4),
                scales=x_scales[:, cols[h]],
                in_=x_grouped[h][:].rearrange("p n j -> p (n j)"),
            )

        def quantize_w(h):
            nc.vector.quantize_mx(
                out=w_codes[:, mcols[h]].bitcast(FP8X4),
                scales=w_scales[:, mcols[h]],
                in_=w_grouped[h][:].rearrange("p n j -> p (n j)"),
            )

        def product(m, h):
            nc.tensor.matmul_mx(
                out=accs[m][h][:],
                lhsT=w_codes[:, mcols[m]].bitcast(FP8X4),
                lhsT_scale=w_scales[:, mcols[m]],
                rhs=x_codes[:, cols[h]].bitcast(FP8X4),
                rhs_scale=x_scales[:, cols[h]],
                start=True,
                stop=True,
            )

        def grouped_sums(m, h):
            return accs[m][h][:].rearrange("p (v d) -> p v d", d=D)

        def w_copy_s(m):
            nc.scalar.copy(
                w_grouped[m][:].rearrange("p (c i) j -> p c j i", i=4),
                w_raw[:, :, mcols[m]].rearrange("p j (c i) -> p c j i", i=4),
            )

        def largest(m, h):
            nc.vector.tensor_reduce(out=pooled[m][:, vcols[h]], in_=grouped_sums(m, h), axis=AXIS_X, op=MAX)

        def finish(m, h):
            nc.scalar.activation(result[m][:, vcols[h]], pooled[m][:, vcols[h]], RELU, bias=bias[:, m : m + 1])

        def store(m):
            nc.sync.dma_start(out[m * P : (m + 1) * P, :], result[m][:])

        gather(0, 0)
        gather(1, 0)
        for t in (2, 3, 1):
            gather(0, t)
            gather(1, t)
        w_copy_s(0)
        w_copy_s(1)
        quantize_x(0)
        quantize_w(0)
        product(0, 0)
        quantize_x(1)
        product(0, 1)
        quantize_w(1)
        nc.tensor.transpose(bias_turned[:], bias_rows[:], identity[:])
        nc.scalar.copy(bias[:], bias_turned[:, 0:2])
        product(1, 0)
        product(1, 1)
        for m in range(2):
            for h in range(2):
                largest(m, h)
                finish(m, h)
            store(m)
